import numpy as np
import ml_dtypes


def mxq(x, axis, fmt="e4m3"):
    dtype, down = {"e4m3": (ml_dtypes.float8_e4m3fn, 7), "e5m2": (ml_dtypes.float8_e5m2, 14)}[fmt]
    v = np.moveaxis(np.asarray(x, np.float32).astype(ml_dtypes.bfloat16).astype(np.float64), axis, -1)
    blocks = v.reshape(v.shape[:-1] + (-1, 32))
    amax = np.abs(blocks).max(-1, keepdims=True)
    byte = np.maximum(np.where(amax > 0, np.frexp(amax)[1] - 1 + 127, 0) - down, 1)
    scale = np.exp2(byte - 127.0)
    codes = (blocks / scale).astype(np.float32).astype(dtype).astype(np.float64)
    return np.moveaxis((codes * scale).reshape(v.shape), -1, axis)


WIDE = False


def mx_kscale(k):
    if not WIDE:
        return np.ones(k)
    levels = np.array([10, -10, 5, -5, 0])
    if k % 512:
        return np.exp2(np.random.permutation(np.resize(levels, k // 32))).repeat(32)
    a = np.empty((k // 512, 16))
    for p in range(k // 512):
        a[p, :8] = np.random.permutation(np.resize(levels, 8))
        for g in range(8):
            far = levels[np.abs(levels - a[p, g]) >= 10]
            a[p, g + 8] = far[np.random.randint(len(far))]
    return np.exp2(a.ravel()).repeat(32)


def f64(x):
    return np.asarray(x).astype(np.float64)


def striped(idx):
    return np.tile(idx.reshape(-1, 16).T, (8, 1)).astype(np.uint16)


def unstriped(offs):
    return offs[:16].T.reshape(-1).astype(np.int64)


E2M1 = np.array([0.0, 0.5, 1.0, 1.5, 2.0, 3.0, 4.0, 6.0, -0.0, -0.5, -1.0, -1.5, -2.0, -3.0, -4.0, -6.0])


def pack_weight(w, fmt):
    k, n = w.shape
    w = f64(np.asarray(w, np.float32).astype(ml_dtypes.bfloat16)).reshape(k // 32, 32, n)
    amax = np.abs(w).max(1)
    if fmt == "e4m3":
        byte = np.frexp(amax)[1] - 1 + 127 - 7
    else:
        mant, ex = np.frexp(amax / 6.0)
        byte = np.where(mant > 0.5, ex, ex - 1) + 127
    byte = np.clip(np.where(amax > 0, byte, 1), 1, 254)
    scaled = (w * np.exp2(127.0 - byte)[:, None, :]).reshape(k, n).astype(np.float32)
    by_word = np.ascontiguousarray(scaled.reshape(k // 512, 128, 4, n).transpose(0, 1, 3, 2))
    if fmt == "e4m3":
        words = by_word.astype(ml_dtypes.float8_e4m3fn).view(np.uint8)
    else:
        c = by_word.astype(ml_dtypes.float4_e2m1fn).view(np.uint8) & 0xF
        words = (c[..., 0::2] | (c[..., 1::2] << 4)).reshape(k // 512, 128, 2 * n)
    return np.ascontiguousarray(words), np.ascontiguousarray(byte.astype(np.uint8).reshape(k // 512, 16, n))


def unpack_weight(words, scales, fmt):
    g, _, n = scales.shape
    words = np.ascontiguousarray(words).reshape(g, 128, n, -1)
    if fmt == "e4m3":
        vals = words.view(ml_dtypes.float8_e4m3fn).astype(np.float64)
    else:
        nib = np.empty((g, 128, n, 4), np.uint8)
        nib[..., 0::2] = words & 0xF
        nib[..., 1::2] = words >> 4
        vals = E2M1[nib]
    vals = vals * np.repeat(np.exp2(scales.astype(np.float64) - 127.0), 8, axis=1)[..., None]
    return vals.transpose(0, 1, 3, 2).reshape(g * 512, n)


def gelu(v):
    return 0.5 * v * (1.0 + np.tanh(np.sqrt(2.0 / np.pi) * (v + 0.044715 * v**3)))


K, H, N, T, S, P = 1536, 1024, 768, 4096, 1024, 512

def setup_inputs():
    n = np.random.standard_normal
    s = mx_kscale(K)[:, None]
    u = mx_kscale(H)[:, None]
    d = {}
    d["tab_words"], d["tab_scales"] = pack_weight(n((K, T)) * s, "e2m1")
    d["offs"] = striped(np.random.permutation(T)[:S])
    d["pos1"] = striped(np.random.permutation(S)[:P])
    d["pos2"] = striped(np.random.permutation(S)[:P])
    d["w1"] = (n((K, H)) / s * u.T / K ** 0.5).astype(np.float32)
    d["base"] = (np.random.uniform(0.1, 0.5, H) * u[:, 0] ** 2).astype(np.float32)
    d["w4_words"], d["w4_scales"] = pack_weight(n((H, N)) / u / H ** 0.5, "e2m1")
    d["slope"] = (0.6 * n((N, P))).astype(np.float32)
    return d

def reference(tab_words, tab_scales, offs, pos1, pos2, w1, base, w4_words, w4_scales, slope):
    v = unpack_weight(tab_words, tab_scales, "e2m1")[:, unstriped(offs)]
    h = mxq(f64(w1), 0, "e4m3").T @ v
    along = h[:, unstriped(pos1)]
    across = h[:, unstriped(pos2)]
    z = np.sqrt(np.square(along) + np.square(across) + f64(base)[:, None])
    w4 = unpack_weight(w4_words, w4_scales, "e2m1")
    y = w4.T @ mxq(z, 0, "e4m3")
    return y - f64(slope)

@@ -1,0 +1,261 @@
+from contextlib import ExitStack
+
+import concourse.mybir as mybir
+
+K, H, N, T, S, M = 1536, 1024, 768, 4096, 1024, 512
+FLOPS = 2 * K * H * S + 2 * H * N * M
+
+F32 = mybir.dt.float32
+BF16 = mybir.dt.bfloat16
+I32 = mybir.dt.int32
+U32 = mybir.dt.uint32
+U16 = mybir.dt.uint16
+U8 = mybir.dt.uint8
+FP8X4 = mybir.dt.float8_e4m3fn_x4
+FP4X4 = mybir.dt.float4_e2m1fn_x4
+ACT = mybir.ActivationFunctionType
+ALU = mybir.AluOpType
+
+P = 128
+PACK = 4
+PASS = P * PACK
+KP = K // PASS
+HP = H // PASS
+BANK = 512
+NT = N // P
+
+
+def tile_list_putt_break_features_kernel(
+    tc, tab_words, tab_scales, offs, pos1, pos2, w1, base, w4_words, w4_scales, slope, out
+):
+    nc = tc.nc
+    with ExitStack() as ctx:
+        keep = ctx.enter_context(tc.tile_pool(name="keep", bufs=1))
+        ring = ctx.enter_context(tc.tile_pool(name="ring", bufs=2))
+        psum = ctx.enter_context(tc.psum_pool(name="psum", bufs=8))
+
+        offs_t = keep.tile([P, S // 16], U16, name="offs_t")
+        pos1_t = keep.tile([P, M // 16], U16, name="pos1_t")
+        pos2_t = keep.tile([P, M // 16], U16, name="pos2_t")
+        tab_t = [keep.tile([P, T], U16, name="tab%d" % a, align_bytes=64) for a in range(KP)]
+        tsc_t = keep.tile([P, T], U8, name="tsc", align_bytes=64)
+        tsc_g = keep.tile([P, S], U8, name="tsc_g", align_bytes=64)
+        v_scales = keep.tile([P, KP, S], U8, name="v_scales", align_bytes=64)
+        v_words = [keep.tile([P, S], U16, name="vw%d" % a, align_bytes=64) for a in range(KP)]
+        w_raw = {}
+        w_codes = {}
+        shared = {("codes", 2, 0): "x0", ("bf", 0, 1): "x0", ("along", 0, 2): "x0", ("bf", 1, 1): "x1", ("along", 0, 3): "x1", ("bf", 2, 1): "x2", ("sums", 0, 3): "x2"}
+        for a in range(KP):
+            for b in range(HP):
+                shared["raw", a, b] = "raw%d" % a
+        shared["w4w", 0, 0] = "raw0"
+        shared["slope", 0, 0] = "raw1"
+
+        def own_tile(kind, i, j, shape, dtype):
+            tag = shared.get((kind, i, j), "%s%d%d" % (kind, i, j))
+            return keep.tile(shape, dtype, name=tag, tag=tag, align_bytes=64)
+
+        w_scales = {}
+        for b in range(HP):
+            for a in range(KP):
+                w_scales[a, b] = keep.tile([P, PASS], U8, name="wsc%d%d" % (a, b), align_bytes=64)
+        base_t = keep.tile([P, HP, PACK], F32, name="base_t")
+        warm = keep.tile([P, 1], F32, name="warm")
+        w4s_t = keep.tile([P, HP, N], U8, name="w4s", align_bytes=64)
+
+        def load_tab(a, pieces=1):
+            width = T // 2 // pieces
+            for i in range(pieces):
+                cols = slice(i * width, (i + 1) * width)
+                nc.sync.dma_start(out=tab_t[a][:].bitcast(I32)[:, cols], in_=tab_words[a].bitcast(I32)[:, cols])
+
+        def load_w(a, b):
+            w_raw[a, b] = own_tile("raw", a, b, [P, PACK, PASS], F32)
+            rows = w1[a * PASS : (a + 1) * PASS, b * PASS : (b + 1) * PASS]
+            nc.sync.dma_start(out=w_raw[a, b][:], in_=rows.rearrange("(p j) c -> p j c", j=PACK))
+
+        nc.gpsimd.memset(tsc_t[:].bitcast(I32), 0)
+        nc.gpsimd.dma_start(
+            out=tsc_t[0:96:2, :].bitcast(I32), in_=tab_scales.rearrange("a q t -> q a t").bitcast(I32)
+        )
+        nc.gpsimd.memset(v_scales[:].rearrange("p a s -> p (a s)").bitcast(I32), 0)
+        nc.gpsimd.memset(w4s_t[:].rearrange("p a s -> p (a s)").bitcast(I32), 0)
+        nc.vector.memset(warm[:], 1.0)
+        nc.scalar.activation(warm[:], warm[:], ACT.Sqrt)
+        for q in range(4):
+            nc.gpsimd.dma_start(
+                out=w4s_t[32 * q : 32 * q + 4, :, :].bitcast(I32),
+                in_=w4_scales[:, 4 * q : 4 * q + 4, :].rearrange("a r c -> r a c").bitcast(I32),
+            )
+
+        nc.sync.dma_start(offs_t[:], offs)
+        load_tab(0, 4)
+        nc.sync.dma_start(pos1_t[:], pos1)
+        nc.sync.dma_start(pos2_t[:], pos2)
+        nc.sync.dma_start(out=base_t[:], in_=base.rearrange("(b p t) -> p b t", p=P, t=PACK))
+        load_w(0, 0)
+        load_tab(1)
+        load_w(1, 0)
+        load_tab(2)
+        load_w(2, 0)
+
+        nc.vector.tensor_copy(tsc_g[:], tsc_t[:].indirect(offs_t[:]))
+        for q in range(4):
+            nc.scalar.dma_start(
+                out=v_scales[32 * q : 32 * q + 4, :, :].rearrange("p a s -> p (a s)").bitcast(I32),
+                in_=tsc_g[24 * q : 24 * q + 24 : 2, :].bitcast(I32),
+            )
+
+        def gather_words(a):
+            nc.vector.tensor_copy(v_words[a][:], tab_t[a][:].indirect(offs_t[:]))
+
+        w_bf = {}
+
+        def cast_w(a, b, vector_cols):
+            w_bf[a, b] = own_tile("bf", a, b, [P, PACK, P, PACK], BF16)
+            src = w_raw[a, b][:].rearrange("p j (m t) -> p m j t", t=PACK)
+            dst = w_bf[a, b][:].rearrange("p t m j -> p m j t")
+            if vector_cols > 0:
+                nc.vector.tensor_copy(dst[:, :vector_cols], src[:, :vector_cols])
+            if vector_cols < P:
+                nc.scalar.copy(dst[:, vector_cols:], src[:, vector_cols:])
+
+        def quant_w(a, b, t0=0, t1=PACK):
+            cols = slice(t0 * P, t1 * P)
+            if t0 == 0:
+                w_codes[a, b] = own_tile("codes", a, b, [P, PASS], U32)
+            nc.vector.quantize_mx(
+                out=w_codes[a, b][:, cols].bitcast(FP8X4),
+                scales=w_scales[a, b][:, cols],
+                in_=w_bf[a, b][:, t0:t1].rearrange("p t m j -> p (t m j)"),
+            )
+
+        h_acc = {}
+
+        def mm_h(a, b, t):
+            cols = slice(t * P, (t + 1) * P)
+            for half in range(S // BANK):
+                if a == 0:
+                    h_acc[b, t, half] = psum.tile([P, BANK], F32, name="acc", tag="acc")
+                sc = slice(half * BANK, (half + 1) * BANK)
+                nc.tensor.matmul_mx(
+                    out=h_acc[b, t, half][:],
+                    lhsT=w_codes[a, b][:, cols].bitcast(FP8X4),
+                    lhsT_scale=w_scales[a, b][:, cols],
+                    rhs=v_words[a][:, sc].bitcast(FP4X4),
+                    rhs_scale=v_scales[:, a, sc],
+                    start=(a == 0),
+                    stop=(a == KP - 1),
+                )
+
+        h_sq = {}
+        sums = {}
+        z_rows = [keep.tile([P, PACK, M], BF16, name="zrows%d" % b, align_bytes=64) for b in range(HP)]
+        z_bf = [keep.tile([P, M, PACK], BF16, name="zbf%d" % b, align_bytes=64) for b in range(HP)]
+        z_codes = [keep.tile([P, M], U32, name="zcod%d" % b, align_bytes=64) for b in range(HP)]
+        z_scales = [keep.tile([P, M], U8, name="zsc%d" % b, align_bytes=64) for b in range(HP)]
+
+        def square_out(b, t):
+            h_sq[b, t] = own_tile("hsq", b, t, [P, S], F32)
+            for half in range(S // BANK):
+                nc.scalar.activation(h_sq[b, t][:, half * BANK : (half + 1) * BANK], h_acc[b, t, half][:], ACT.Square)
+
+        def pick(b, t):
+            along = own_tile("along", b, t, [P, M], F32)
+            sums[b, t] = own_tile("sums", b, t, [P, M], F32)
+            nc.vector.tensor_copy(along[:], h_sq[b, t][:].indirect(pos1_t[:]))
+            nc.vector.tensor_tensor(sums[b, t][:], h_sq[b, t][:].indirect(pos2_t[:]), along[:], ALU.add)
+
+        def root(b, t):
+            nc.scalar.activation(z_rows[b][:, t, :], sums[b, t][:], ACT.Sqrt, bias=base_t[:, b, t : t + 1])
+
+        def weave(b, on_vector):
+            src = z_rows[b][:].rearrange("p t (c i) -> p c t i", i=4)
+            dst = z_bf[b][:].rearrange("p (c i) t -> p c t i", i=4)
+            if on_vector:
+                nc.vector.tensor_copy(dst, src)
+            else:
+                nc.scalar.copy(dst, src)
+
+        def quant_z(b):
+            nc.vector.quantize_mx(
+                out=z_codes[b][:].bitcast(FP8X4),
+                scales=z_scales[b][:],
+                in_=z_bf[b][:].rearrange("p m t -> p (m t)"),
+            )
+
+        y_acc = {}
+
+        def mm_y(b, n):
+            if b == 0:
+                y_acc[n] = psum.tile([P, BANK], F32, name="acc", tag="acc")
+            nc.tensor.matmul_mx(
+                out=y_acc[n][:],
+                lhsT=w4w_t[:, b, 2 * n * P : 2 * (n + 1) * P].bitcast(FP4X4),
+                lhsT_scale=w4s_t[:, b, n * P : (n + 1) * P],
+                rhs=z_codes[b][:].bitcast(FP8X4),
+                rhs_scale=z_scales[b][:],
+                start=(b == 0),
+                stop=(b == HP - 1),
+            )
+
+        for a in range(KP):
+            gather_words(a)
+            cast_w(a, 0, (84, 64, 76)[a])
+            load_w(a, 1)
+            if a < KP - 1:
+                quant_w(a, 0)
+            else:
+                quant_w(a, 0, 0, 1)
+                quant_w(a, 0, 1, 2)
+                quant_w(a, 0, 2, 4)
+            for t in range(PACK):
+                mm_h(a, 0, t)
+
+        square_out(0, 0)
+        square_out(0, 1)
+        pick(0, 0)
+        pick(0, 1)
+        cast_w(0, 1, 0)
+        w4w_t = own_tile("w4w", 0, 0, [P, HP, 2 * N], U8)
+        nc.sync.dma_start(out=w4w_t[:].bitcast(I32), in_=w4_words.rearrange("a p c -> p a c").bitcast(I32))
+        quant_w(0, 1)
+        square_out(0, 2)
+        pick(0, 2)
+        cast_w(1, 1, 0)
+        slope_t = own_tile("slope", 0, 0, [P, NT, M], F32)
+        nc.sync.dma_start(out=slope_t[:], in_=slope.rearrange("(n p) m -> p n m", p=P))
+        quant_w(1, 1)
+        square_out(0, 3)
+        for t in range(2):
+            mm_h(0, 1, t)
+            mm_h(1, 1, t)
+        cast_w(2, 1, 48)
+        quant_w(2, 1)
+        for t in range(2):
+            mm_h(2, 1, t)
+        for t in range(2, PACK):
+            for a in range(KP):
+                mm_h(a, 1, t)
+        pick(0, 3)
+        square_out(1, 0)
+        square_out(1, 1)
+        for t in range(PACK):
+            root(0, t)
+        square_out(1, 2)
+        square_out(1, 3)
+        for t in range(PACK):
+            pick(1, t)
+        weave(0, False)
+        quant_z(0)
+        for n in range(NT):
+            mm_y(0, n)
+        for t in range(PACK):
+            root(1, t)
+        weave(1, True)
+        quant_z(1)
+        for n in range(NT):
+            mm_y(1, n)
+            res = ring.tile([P, M], F32, name="res", tag="res", bufs=NT, align_bytes=64)
+            nc.vector.tensor_tensor(res[:], y_acc[n][:], slope_t[:, n, :], ALU.subtract)
+            nc.sync.dma_start(out=out[n * P : (n + 1) * P, :], in_=res[:])

@@ -23,6 +23,7 @@ KP = K // PASS
 HP = H // PASS
 BANK = 512
 NT = N // P
+HM = M // 2
 
 
 def tile_list_putt_break_features_kernel(
@@ -31,85 +32,81 @@ def tile_list_putt_break_features_kernel(
     nc = tc.nc
     with ExitStack() as ctx:
         keep = ctx.enter_context(tc.tile_pool(name="keep", bufs=1))
-        ring = ctx.enter_context(tc.tile_pool(name="ring", bufs=2))
         psum = ctx.enter_context(tc.psum_pool(name="psum", bufs=8))
 
         offs_t = keep.tile([P, S // 16], U16, name="offs_t")
         pos1_t = keep.tile([P, M // 16], U16, name="pos1_t")
         pos2_t = keep.tile([P, M // 16], U16, name="pos2_t")
-        tab_t = [keep.tile([P, T], U16, name="tab%d" % a, align_bytes=64) for a in range(KP)]
-        tsc_t = keep.tile([P, T], U8, name="tsc", align_bytes=64)
-        tsc_g = keep.tile([P, S], U8, name="tsc_g", align_bytes=64)
-        v_scales = keep.tile([P, KP, S], U8, name="v_scales", align_bytes=64)
-        v_words = [keep.tile([P, S], U16, name="vw%d" % a, align_bytes=64) for a in range(KP)]
-        w_raw = {}
-        w_codes = {}
-        shared = {("codes", 2, 0): "x0", ("bf", 0, 1): "x0", ("along", 0, 2): "x0", ("bf", 1, 1): "x1", ("along", 0, 3): "x1", ("bf", 2, 1): "x2", ("sums", 0, 3): "x2"}
-        for a in range(KP):
-            for b in range(HP):
-                shared["raw", a, b] = "raw%d" % a
-        shared["w4w", 0, 0] = "raw0"
-        shared["slope", 0, 0] = "raw1"
+        chains = [
+            [("tsc", 0, 0), ("tab", 2, 0), ("raw", 0, 1), ("slope", 0, 0)],
+            [("warm", 0, 0), ("tab", 0, 0), ("raw", 1, 0), ("raw", 1, 1), ("w4w", 0, 0)],
+            [("warm", 1, 0), ("tab", 1, 0), ("raw", 2, 0), ("raw", 2, 1)],
+            [("codes", 2, 0), ("bf", 0, 1)],
+            [("codes", 2, 1), ("zbf", 0, 0)],
+            [("wsc", 2, 1), ("zbf", 0, 1)],
+            [("basew", 1, 0), ("sums", 1, 1)],
+        ]
+        shared = {}
+        for i, chain in enumerate(chains):
+            for key in chain:
+                shared[key] = "chain%d" % i
 
         def own_tile(kind, i, j, shape, dtype):
             tag = shared.get((kind, i, j), "%s%d%d" % (kind, i, j))
             return keep.tile(shape, dtype, name=tag, tag=tag, align_bytes=64)
 
-        w_scales = {}
-        for b in range(HP):
-            for a in range(KP):
-                w_scales[a, b] = keep.tile([P, PASS], U8, name="wsc%d%d" % (a, b), align_bytes=64)
-        base_t = keep.tile([P, HP, PACK], F32, name="base_t")
-        warm = keep.tile([P, 1], F32, name="warm")
-        w4s_t = keep.tile([P, HP, N], U8, name="w4s", align_bytes=64)
+        tab_t, w_raw, w_bf, w_codes, w_scales = {}, {}, {}, {}, {}
+        tsc_t = own_tile("tsc", 0, 0, [P, T], U8)
+        tsc_g = own_tile("tscg", 0, 0, [P, S], U8)
+        v_scales = own_tile("vsc", 0, 0, [P, KP * S], U8)
+        w4s_t = own_tile("w4s", 0, 0, [P, HP, N], U8)
+        v_words = [own_tile("vw", a, 0, [P, S], U16) for a in range(KP)]
+        base_t = own_tile("base", 0, 0, [P, HP, PACK], F32)
+        warm_in = own_tile("warm", 0, 0, [P, 1], F32)
+        warm_out = own_tile("warm", 1, 0, [P, 1], F32)
 
-        def load_tab(a, pieces=1):
-            width = T // 2 // pieces
-            for i in range(pieces):
-                cols = slice(i * width, (i + 1) * width)
-                nc.sync.dma_start(out=tab_t[a][:].bitcast(I32)[:, cols], in_=tab_words[a].bitcast(I32)[:, cols])
+        def load_tab(a):
+            tab_t[a] = own_tile("tab", a, 0, [P, T], U16)
+            nc.sync.dma_start(out=tab_t[a][:].bitcast(I32), in_=tab_words[a].bitcast(I32))
 
         def load_w(a, b):
             w_raw[a, b] = own_tile("raw", a, b, [P, PACK, PASS], F32)
             rows = w1[a * PASS : (a + 1) * PASS, b * PASS : (b + 1) * PASS]
             nc.sync.dma_start(out=w_raw[a, b][:], in_=rows.rearrange("(p j) c -> p j c", j=PACK))
 
-        nc.gpsimd.memset(tsc_t[:].bitcast(I32), 0)
-        nc.gpsimd.dma_start(
+        nc.vector.memset(tsc_t[:].bitcast(I32), 0)
+        nc.gpsimd.memset(warm_in[:], 1.0)
+        nc.scalar.activation(warm_out[:], warm_in[:], ACT.Sqrt)
+
+        nc.sync.dma_start(offs_t[:], offs)
+        load_w(0, 0)
+        nc.sync.dma_start(
             out=tsc_t[0:96:2, :].bitcast(I32), in_=tab_scales.rearrange("a q t -> q a t").bitcast(I32)
         )
-        nc.gpsimd.memset(v_scales[:].rearrange("p a s -> p (a s)").bitcast(I32), 0)
-        nc.gpsimd.memset(w4s_t[:].rearrange("p a s -> p (a s)").bitcast(I32), 0)
-        nc.vector.memset(warm[:], 1.0)
-        nc.scalar.activation(warm[:], warm[:], ACT.Sqrt)
+        nc.sync.dma_start(pos1_t[:], pos1)
+        nc.sync.dma_start(pos2_t[:], pos2)
+        nc.gpsimd.dma_start(out=base_t[:], in_=base.rearrange("(b p t) -> p b t", p=P, t=PACK))
+        nc.gpsimd.memset(v_scales[:].bitcast(I32), 0)
+        nc.gpsimd.memset(w4s_t[:].rearrange("p a c -> p (a c)").bitcast(I32), 0)
         for q in range(4):
             nc.gpsimd.dma_start(
                 out=w4s_t[32 * q : 32 * q + 4, :, :].bitcast(I32),
                 in_=w4_scales[:, 4 * q : 4 * q + 4, :].rearrange("a r c -> r a c").bitcast(I32),
             )
-
-        nc.sync.dma_start(offs_t[:], offs)
-        load_tab(0, 4)
-        nc.sync.dma_start(pos1_t[:], pos1)
-        nc.sync.dma_start(pos2_t[:], pos2)
-        nc.sync.dma_start(out=base_t[:], in_=base.rearrange("(b p t) -> p b t", p=P, t=PACK))
-        load_w(0, 0)
+        load_tab(0)
         load_tab(1)
-        load_w(1, 0)
-        load_tab(2)
-        load_w(2, 0)
 
         nc.vector.tensor_copy(tsc_g[:], tsc_t[:].indirect(offs_t[:]))
         for q in range(4):
-            nc.scalar.dma_start(
-                out=v_scales[32 * q : 32 * q + 4, :, :].rearrange("p a s -> p (a s)").bitcast(I32),
+            queue = nc.sync if q < 2 else nc.scalar
+            queue.dma_start(
+                out=v_scales[32 * q : 32 * q + 4, :].bitcast(I32),
                 in_=tsc_g[24 * q : 24 * q + 24 : 2, :].bitcast(I32),
             )
+        load_tab(2)
 
         def gather_words(a):
             nc.vector.tensor_copy(v_words[a][:], tab_t[a][:].indirect(offs_t[:]))
-
-        w_bf = {}
 
         def cast_w(a, b, vector_cols):
             w_bf[a, b] = own_tile("bf", a, b, [P, PACK, P, PACK], BF16)
@@ -124,6 +121,7 @@ def tile_list_putt_break_features_kernel(
             cols = slice(t0 * P, t1 * P)
             if t0 == 0:
                 w_codes[a, b] = own_tile("codes", a, b, [P, PASS], U32)
+                w_scales[a, b] = own_tile("wsc", a, b, [P, PASS], U8)
             nc.vector.quantize_mx(
                 out=w_codes[a, b][:, cols].bitcast(FP8X4),
                 scales=w_scales[a, b][:, cols],
@@ -137,125 +135,154 @@ def tile_list_putt_break_features_kernel(
             for half in range(S // BANK):
                 if a == 0:
                     h_acc[b, t, half] = psum.tile([P, BANK], F32, name="acc", tag="acc")
-                sc = slice(half * BANK, (half + 1) * BANK)
                 nc.tensor.matmul_mx(
                     out=h_acc[b, t, half][:],
                     lhsT=w_codes[a, b][:, cols].bitcast(FP8X4),
                     lhsT_scale=w_scales[a, b][:, cols],
-                    rhs=v_words[a][:, sc].bitcast(FP4X4),
-                    rhs_scale=v_scales[:, a, sc],
+                    rhs=v_words[a][:, half * BANK : (half + 1) * BANK].bitcast(FP4X4),
+                    rhs_scale=v_scales[:, a * S + half * BANK : a * S + (half + 1) * BANK],
                     start=(a == 0),
                     stop=(a == KP - 1),
                 )
 
-        h_sq = {}
-        sums = {}
-        z_rows = [keep.tile([P, PACK, M], BF16, name="zrows%d" % b, align_bytes=64) for b in range(HP)]
-        z_bf = [keep.tile([P, M, PACK], BF16, name="zbf%d" % b, align_bytes=64) for b in range(HP)]
-        z_codes = [keep.tile([P, M], U32, name="zcod%d" % b, align_bytes=64) for b in range(HP)]
-        z_scales = [keep.tile([P, M], U8, name="zsc%d" % b, align_bytes=64) for b in range(HP)]
+        base_w, h_sq, along, sums, z_bf, z_codes, z_scales = {}, {}, {}, {}, {}, {}, {}
+
+        def spread_base(b):
+            base_w[b] = own_tile("basew", b, 0, [P, PACK, HM], F32)
+            nc.scalar.copy(base_w[b][:], base_t[:, b, :].unsqueeze(2).to_broadcast([P, PACK, HM]))
 
         def square_out(b, t):
             h_sq[b, t] = own_tile("hsq", b, t, [P, S], F32)
             for half in range(S // BANK):
                 nc.scalar.activation(h_sq[b, t][:, half * BANK : (half + 1) * BANK], h_acc[b, t, half][:], ACT.Square)
 
-        def pick(b, t):
-            along = own_tile("along", b, t, [P, M], F32)
-            sums[b, t] = own_tile("sums", b, t, [P, M], F32)
-            nc.vector.tensor_copy(along[:], h_sq[b, t][:].indirect(pos1_t[:]))
-            nc.vector.tensor_tensor(sums[b, t][:], h_sq[b, t][:].indirect(pos2_t[:]), along[:], ALU.add)
+        def pick_along(b, t):
+            along[b, t] = own_tile("along", b, t, [P, M], F32)
+            for i in range(2):
+                window = h_sq[b, t][:].indirect(pos1_t[:, i * HM // 16 : (i + 1) * HM // 16])
+                nc.vector.tensor_tensor(along[b, t][:, i * HM : (i + 1) * HM], window, base_w[b][:, t, :], ALU.add)
 
-        def root(b, t):
-            nc.scalar.activation(z_rows[b][:, t, :], sums[b, t][:], ACT.Sqrt, bias=base_t[:, b, t : t + 1])
+        def pick_across(b, t, i):
+            if t == 0:
+                sums[b, i] = own_tile("sums", b, i, [P, PACK, HM], F32)
+            window = h_sq[b, t][:].indirect(pos2_t[:, i * HM // 16 : (i + 1) * HM // 16])
+            nc.vector.tensor_tensor(sums[b, i][:, t, :], window, along[b, t][:, i * HM : (i + 1) * HM], ALU.add)
 
-        def weave(b, on_vector):
-            src = z_rows[b][:].rearrange("p t (c i) -> p c t i", i=4)
-            dst = z_bf[b][:].rearrange("p (c i) t -> p c t i", i=4)
-            if on_vector:
-                nc.vector.tensor_copy(dst, src)
-            else:
-                nc.scalar.copy(dst, src)
+        def root(b, i):
+            z_bf[b, i] = own_tile("zbf", b, i, [P, HM, PACK], BF16)
+            nc.scalar.activation(
+                z_bf[b, i][:].rearrange("p (c u) t -> p c t u", u=4),
+                sums[b, i][:].rearrange("p t (c u) -> p c t u", u=4),
+                ACT.Sqrt,
+            )
 
-        def quant_z(b):
+        def quant_z(b, i):
+            z_codes[b, i] = own_tile("zcod", b, i, [P, HM], U32)
+            z_scales[b, i] = own_tile("zsc", b, i, [P, HM], U8)
             nc.vector.quantize_mx(
-                out=z_codes[b][:].bitcast(FP8X4),
-                scales=z_scales[b][:],
-                in_=z_bf[b][:].rearrange("p m t -> p (m t)"),
+                out=z_codes[b, i][:].bitcast(FP8X4),
+                scales=z_scales[b, i][:],
+                in_=z_bf[b, i][:].rearrange("p m t -> p (m t)"),
             )
 
         y_acc = {}
 
-        def mm_y(b, n):
+        def mm_y(b, i, g):
             if b == 0:
-                y_acc[n] = psum.tile([P, BANK], F32, name="acc", tag="acc")
-            nc.tensor.matmul_mx(
-                out=y_acc[n][:],
-                lhsT=w4w_t[:, b, 2 * n * P : 2 * (n + 1) * P].bitcast(FP4X4),
-                lhsT_scale=w4s_t[:, b, n * P : (n + 1) * P],
-                rhs=z_codes[b][:].bitcast(FP8X4),
-                rhs_scale=z_scales[b][:],
-                start=(b == 0),
-                stop=(b == HP - 1),
-            )
+                y_acc[i, g] = psum.tile([P, 2, HM], F32, name="acc", tag="acc")
+            for u in range(2):
+                n = 2 * g + u
+                for c in range(HM // P):
+                    cols = slice(c * P, (c + 1) * P)
+                    nc.tensor.matmul_mx(
+                        out=y_acc[i, g][:, u, cols],
+                        lhsT=w4w_t[:, b, 2 * n * P : 2 * (n + 1) * P].bitcast(FP4X4),
+                        lhsT_scale=w4s_t[:, b, n * P : (n + 1) * P],
+                        rhs=z_codes[b, i][:, cols].bitcast(FP8X4),
+                        rhs_scale=z_scales[b, i][:, cols],
+                        start=(b == 0 and u == 0 and c == 0),
+                        stop=(b == HP - 1 and u == 1 and c == HM // P - 1),
+                    )
 
-        for a in range(KP):
-            gather_words(a)
-            cast_w(a, 0, (84, 64, 76)[a])
-            load_w(a, 1)
-            if a < KP - 1:
-                quant_w(a, 0)
-            else:
-                quant_w(a, 0, 0, 1)
-                quant_w(a, 0, 1, 2)
-                quant_w(a, 0, 2, 4)
-            for t in range(PACK):
-                mm_h(a, 0, t)
+        def finish(i, g):
+            ms = slice(i * HM, (i + 1) * HM)
+            res = own_tile("res", i, g, [P, 2, HM], F32)
+            nc.vector.tensor_tensor(res[:], y_acc[i, g][:], slope_t[:, 2 * g : 2 * g + 2, ms], ALU.subtract)
+            rows = out[2 * g * P : (2 * g + 2) * P, ms]
+            nc.sync.dma_start(out=rows.rearrange("(u p) m -> p u m", p=P), in_=res[:])
+
+        cast_w(0, 0, 0)
+        gather_words(0)
+        load_w(1, 0)
+        quant_w(0, 0)
+        spread_base(0)
+        spread_base(1)
+        gather_words(1)
+        load_w(2, 0)
+        for t in range(PACK):
+            mm_h(0, 0, t)
+        gather_words(2)
+        load_w(0, 1)
+        cast_w(1, 0, 84)
+        load_w(1, 1)
+        quant_w(1, 0)
+        cast_w(2, 0, 84)
+        load_w(2, 1)
+        quant_w(2, 0, 0, 1)
+        quant_w(2, 0, 1, 2)
+        quant_w(2, 0, 2, 4)
+        for t in range(PACK):
+            mm_h(1, 0, t)
+            mm_h(2, 0, t)
+
+        def pick_first(t):
+            pick_along(0, t)
+            pick_across(0, t, 0)
+            pick_across(0, t, 1)
 
         square_out(0, 0)
+        pick_first(0)
         square_out(0, 1)
-        pick(0, 0)
-        pick(0, 1)
+        pick_first(1)
         cast_w(0, 1, 0)
-        w4w_t = own_tile("w4w", 0, 0, [P, HP, 2 * N], U8)
-        nc.sync.dma_start(out=w4w_t[:].bitcast(I32), in_=w4_words.rearrange("a p c -> p a c").bitcast(I32))
-        quant_w(0, 1)
-        square_out(0, 2)
-        pick(0, 2)
-        cast_w(1, 1, 0)
         slope_t = own_tile("slope", 0, 0, [P, NT, M], F32)
         nc.sync.dma_start(out=slope_t[:], in_=slope.rearrange("(n p) m -> p n m", p=P))
+        quant_w(0, 1)
+        square_out(0, 2)
+        pick_first(2)
+        cast_w(1, 1, 0)
+        w4w_t = own_tile("w4w", 0, 0, [P, HP, 2 * N], U8)
+        nc.sync.dma_start(out=w4w_t[:].bitcast(I32), in_=w4_words.rearrange("a p c -> p a c").bitcast(I32))
         quant_w(1, 1)
-        square_out(0, 3)
-        for t in range(2):
-            mm_h(0, 1, t)
-            mm_h(1, 1, t)
-        cast_w(2, 1, 48)
+        cast_w(2, 1, 64)
         quant_w(2, 1)
-        for t in range(2):
-            mm_h(2, 1, t)
-        for t in range(2, PACK):
+        square_out(0, 3)
+        pick_first(3)
+        for t in range(PACK):
             for a in range(KP):
                 mm_h(a, 1, t)
-        pick(0, 3)
-        square_out(1, 0)
-        square_out(1, 1)
         for t in range(PACK):
-            root(0, t)
-        square_out(1, 2)
-        square_out(1, 3)
+            square_out(1, t)
+            pick_along(1, t)
+            pick_across(1, t, 0)
+            if t == 1:
+                for i in range(2):
+                    root(0, i)
+                    quant_z(0, i)
+        for i in range(2):
+            for g in range(NT // 2):
+                mm_y(0, i, g)
+        root(1, 0)
+        quant_z(1, 0)
         for t in range(PACK):
-            pick(1, t)
-        weave(0, False)
-        quant_z(0)
-        for n in range(NT):
-            mm_y(0, n)
-        for t in range(PACK):
-            root(1, t)
-        weave(1, True)
-        quant_z(1)
-        for n in range(NT):
-            mm_y(1, n)
-            res = ring.tile([P, M], F32, name="res", tag="res", bufs=NT, align_bytes=64)
-            nc.vector.tensor_tensor(res[:], y_acc[n][:], slope_t[:, n, :], ALU.subtract)
-            nc.sync.dma_start(out=out[n * P : (n + 1) * P, :], in_=res[:])
+            pick_across(1, t, 1)
+        root(1, 1)
+        for g in range(NT // 2):
+            mm_y(1, 0, g)
+        finish(0, 0)
+        quant_z(1, 1)
+        finish(0, 1)
+        finish(0, 2)
+        for g in range(NT // 2):
+            mm_y(1, 1, g)
+            finish(1, g)

@@ -32,19 +32,24 @@ def tile_list_putt_break_features_kernel(
     nc = tc.nc
     with ExitStack() as ctx:
         keep = ctx.enter_context(tc.tile_pool(name="keep", bufs=1))
+        stream = ctx.enter_context(tc.tile_pool(name="stream", bufs=1))
         psum = ctx.enter_context(tc.psum_pool(name="psum", bufs=8))
 
         offs_t = keep.tile([P, S // 16], U16, name="offs_t")
         pos1_t = keep.tile([P, M // 16], U16, name="pos1_t")
         pos2_t = keep.tile([P, M // 16], U16, name="pos2_t")
+        KB = 1024
+        placed = {
+            ("warm", 0, 0): 0, ("tab", 0, 0): 0, ("warm", 1, 0): 16 * KB - 64, ("tab", 1, 0): 8 * KB, ("raw", 1, 0): 16 * KB,
+            ("tsc", 0, 0): 24 * KB, ("tab", 2, 0): 24 * KB, ("raw", 2, 0): 32 * KB,
+            ("raw", 0, 1): 36 * KB, ("raw", 1, 1): 40 * KB, ("raw", 2, 1): 44 * KB,
+            ("raw", 0, 2): 48 * KB, ("raw", 1, 2): 56 * KB, ("raw", 2, 2): 64 * KB,
+            ("slope", 0, 0): 36 * KB, ("w4w", 0, 0): 56 * KB, ("dealt", 0, 0): 48 * KB,
+        }
         chains = [
-            [("tsc", 0, 0), ("tab", 2, 0), ("raw", 0, 1), ("slope", 0, 0)],
-            [("warm", 0, 0), ("tab", 0, 0), ("raw", 1, 0), ("raw", 1, 1), ("w4w", 0, 0)],
-            [("warm", 1, 0), ("tab", 1, 0), ("raw", 2, 0), ("raw", 2, 1)],
-            [("codes", 2, 0), ("bf", 0, 1)],
-            [("codes", 2, 1), ("zbf", 0, 0)],
-            [("wsc", 2, 1), ("zbf", 0, 1)],
-            [("basew", 1, 0), ("sums", 1, 1)],
+            [("codes", 2, 1), ("bf", 0, 2), ("along", 0, 2)],
+            [("wsc", 2, 1), ("bf", 1, 2), ("nsum", 2, 0)],
+            [("zbf", 0, 0), ("sums", 1, 1)],
         ]
         shared = {}
         for i, chain in enumerate(chains):
@@ -52,42 +57,53 @@ def tile_list_putt_break_features_kernel(
                 shared[key] = "chain%d" % i
 
         def own_tile(kind, i, j, shape, dtype):
-            tag = shared.get((kind, i, j), "%s%d%d" % (kind, i, j))
+            name = "%s%d%d" % (kind, i, j)
+            if (kind, i, j) in placed:
+                return stream.tile(shape, dtype, name=name, tag=name, align_bytes=64, offset=placed[kind, i, j])
+            tag = shared.get((kind, i, j), name)
             return keep.tile(shape, dtype, name=tag, tag=tag, align_bytes=64)
 
+        first_col = (0, 256, 512)
+        deal = (2, 2, 4)
+        tiles = [(0, 0), (0, 1), (1, 0), (1, 1), (2, 0), (2, 1), (2, 2), (2, 3)]
+
         tab_t, w_raw, w_bf, w_codes, w_scales = {}, {}, {}, {}, {}
-        tsc_t = own_tile("tsc", 0, 0, [P, T], U8)
+        tsc_t = own_tile("tsc", 0, 0, [P, 48 * KB], U8)
         tsc_g = own_tile("tscg", 0, 0, [P, S], U8)
         v_scales = own_tile("vsc", 0, 0, [P, KP * S], U8)
         w4s_t = own_tile("w4s", 0, 0, [P, HP, N], U8)
         v_words = [own_tile("vw", a, 0, [P, S], U16) for a in range(KP)]
-        base_t = own_tile("base", 0, 0, [P, HP, PACK], F32)
-        warm_in = own_tile("warm", 0, 0, [P, 1], F32)
-        warm_out = own_tile("warm", 1, 0, [P, 1], F32)
+        base_t = [own_tile("base", b, 0, [P, PACK], F32) for b in range(HP)]
+        warm_in = own_tile("warm", 0, 0, [P, 32], F32)
+        warm_out = own_tile("warm", 1, 0, [P, 32], F32)
 
         def load_tab(a):
             tab_t[a] = own_tile("tab", a, 0, [P, T], U16)
             nc.sync.dma_start(out=tab_t[a][:].bitcast(I32), in_=tab_words[a].bitcast(I32))
 
-        def load_w(a, b):
-            w_raw[a, b] = own_tile("raw", a, b, [P, PACK, PASS], F32)
-            rows = w1[a * PASS : (a + 1) * PASS, b * PASS : (b + 1) * PASS]
-            nc.sync.dma_start(out=w_raw[a, b][:], in_=rows.rearrange("(p j) c -> p j c", j=PACK))
+        def load_w(a, g):
+            width = deal[g] * P
+            w_raw[a, g] = own_tile("raw", a, g, [P, PACK, width], F32)
+            rows = w1[a * PASS : (a + 1) * PASS, first_col[g] : first_col[g] + width]
+            nc.sync.dma_start(out=w_raw[a, g][:], in_=rows.rearrange("(p j) c -> p j c", j=PACK))
 
-        nc.vector.memset(tsc_t[:].bitcast(I32), 0)
+        nc.vector.memset(tsc_t[:, :T].bitcast(I32), 0)
+        nc.vector.memset(v_scales[:].bitcast(I32), 0)
+        nc.vector.memset(w4s_t[:].rearrange("p a c -> p (a c)").bitcast(I32), 0)
         nc.gpsimd.memset(warm_in[:], 1.0)
         nc.scalar.activation(warm_out[:], warm_in[:], ACT.Sqrt)
 
         nc.sync.dma_start(offs_t[:], offs)
         load_w(0, 0)
         nc.sync.dma_start(
-            out=tsc_t[0:96:2, :].bitcast(I32), in_=tab_scales.rearrange("a q t -> q a t").bitcast(I32)
+            out=tsc_t[0:96:2, :T].bitcast(I32), in_=tab_scales.rearrange("a q t -> q a t").bitcast(I32)
         )
         nc.sync.dma_start(pos1_t[:], pos1)
         nc.sync.dma_start(pos2_t[:], pos2)
-        nc.gpsimd.dma_start(out=base_t[:], in_=base.rearrange("(b p t) -> p b t", p=P, t=PACK))
-        nc.gpsimd.memset(v_scales[:].bitcast(I32), 0)
-        nc.gpsimd.memset(w4s_t[:].rearrange("p a c -> p (a c)").bitcast(I32), 0)
+        nc.scalar.dma_start(
+            out=base_t[0][:].rearrange("p (g u) -> p g u", u=2), in_=base[:PASS].rearrange("(g p u) -> p g u", p=P, u=2)
+        )
+        nc.scalar.dma_start(out=base_t[1][:], in_=base[PASS:].rearrange("(p t) -> p t", t=PACK))
         for q in range(4):
             nc.gpsimd.dma_start(
                 out=w4s_t[32 * q : 32 * q + 4, :, :].bitcast(I32),
@@ -95,8 +111,9 @@ def tile_list_putt_break_features_kernel(
             )
         load_tab(0)
         load_tab(1)
+        load_w(1, 0)
 
-        nc.vector.tensor_copy(tsc_g[:], tsc_t[:].indirect(offs_t[:]))
+        nc.vector.tensor_copy(tsc_g[:], tsc_t[:, :T].indirect(offs_t[:]))
         for q in range(4):
             queue = nc.sync if q < 2 else nc.scalar
             queue.dma_start(
@@ -104,41 +121,50 @@ def tile_list_putt_break_features_kernel(
                 in_=tsc_g[24 * q : 24 * q + 24 : 2, :].bitcast(I32),
             )
         load_tab(2)
+        load_w(2, 0)
+        for g in range(1, 3):
+            for a in range(KP):
+                load_w(a, g)
 
         def gather_words(a):
             nc.vector.tensor_copy(v_words[a][:], tab_t[a][:].indirect(offs_t[:]))
 
-        def cast_w(a, b, vector_cols):
-            w_bf[a, b] = own_tile("bf", a, b, [P, PACK, P, PACK], BF16)
-            src = w_raw[a, b][:].rearrange("p j (m t) -> p m j t", t=PACK)
-            dst = w_bf[a, b][:].rearrange("p t m j -> p m j t")
-            if vector_cols > 0:
-                nc.vector.tensor_copy(dst[:, :vector_cols], src[:, :vector_cols])
-            if vector_cols < P:
-                nc.scalar.copy(dst[:, vector_cols:], src[:, vector_cols:])
+        def cast_w(a, g, vector_share):
+            d = deal[g]
+            w_bf[a, g] = own_tile("bf", a, g, [P, d, P, PACK], BF16)
+            src = w_raw[a, g][:].rearrange("p j (c i t) -> p c j i t", i=PACK // d, t=d)
+            dst = w_bf[a, g][:].rearrange("p t (c i) j -> p c j i t", i=PACK // d)
+            if d == PACK:
+                src = w_raw[a, g][:].rearrange("p j (c t) -> p c j t", t=d)
+                dst = w_bf[a, g][:].rearrange("p t c j -> p c j t")
+            runs = P * d // PACK
+            split = 2 * round(runs * vector_share / 2)
+            if split > 0:
+                nc.vector.tensor_copy(dst[:, :split], src[:, :split])
+            if split < runs:
+                nc.scalar.copy(dst[:, split:], src[:, split:])
 
-        def quant_w(a, b, t0=0, t1=PACK):
-            cols = slice(t0 * P, t1 * P)
-            if t0 == 0:
-                w_codes[a, b] = own_tile("codes", a, b, [P, PASS], U32)
-                w_scales[a, b] = own_tile("wsc", a, b, [P, PASS], U8)
+        def quant_w(a, g):
+            w_codes[a, g] = own_tile("codes", a, g, [P, deal[g] * P], U32)
+            w_scales[a, g] = own_tile("wsc", a, g, [P, deal[g] * P], U8)
             nc.vector.quantize_mx(
-                out=w_codes[a, b][:, cols].bitcast(FP8X4),
-                scales=w_scales[a, b][:, cols],
-                in_=w_bf[a, b][:, t0:t1].rearrange("p t m j -> p (t m j)"),
+                out=w_codes[a, g][:].bitcast(FP8X4),
+                scales=w_scales[a, g][:],
+                in_=w_bf[a, g][:].rearrange("p t m j -> p (t m j)"),
             )
 
         h_acc = {}
 
-        def mm_h(a, b, t):
+        def mm_h(a, k):
+            g, t = tiles[k]
             cols = slice(t * P, (t + 1) * P)
             for half in range(S // BANK):
                 if a == 0:
-                    h_acc[b, t, half] = psum.tile([P, BANK], F32, name="acc", tag="acc")
+                    h_acc[k, half] = psum.tile([P, BANK], F32, name="acc", tag="acc")
                 nc.tensor.matmul_mx(
-                    out=h_acc[b, t, half][:],
-                    lhsT=w_codes[a, b][:, cols].bitcast(FP8X4),
-                    lhsT_scale=w_scales[a, b][:, cols],
+                    out=h_acc[k, half][:],
+                    lhsT=w_codes[a, g][:, cols].bitcast(FP8X4),
+                    lhsT_scale=w_scales[a, g][:, cols],
                     rhs=v_words[a][:, half * BANK : (half + 1) * BANK].bitcast(FP4X4),
                     rhs_scale=v_scales[:, a * S + half * BANK : a * S + (half + 1) * BANK],
                     start=(a == 0),
@@ -149,12 +175,12 @@ def tile_list_putt_break_features_kernel(
 
         def spread_base(b):
             base_w[b] = own_tile("basew", b, 0, [P, PACK, HM], F32)
-            nc.scalar.copy(base_w[b][:], base_t[:, b, :].unsqueeze(2).to_broadcast([P, PACK, HM]))
+            nc.scalar.copy(base_w[b][:], base_t[b][:].unsqueeze(2).to_broadcast([P, PACK, HM]))
 
         def square_out(b, t):
             h_sq[b, t] = own_tile("hsq", b, t, [P, S], F32)
             for half in range(S // BANK):
-                nc.scalar.activation(h_sq[b, t][:, half * BANK : (half + 1) * BANK], h_acc[b, t, half][:], ACT.Square)
+                nc.scalar.activation(h_sq[b, t][:, half * BANK : (half + 1) * BANK], h_acc[PACK * b + t, half][:], ACT.Square)
 
         def pick_along(b, t):
             along[b, t] = own_tile("along", b, t, [P, M], F32)
@@ -168,22 +194,38 @@ def tile_list_putt_break_features_kernel(
             window = h_sq[b, t][:].indirect(pos2_t[:, i * HM // 16 : (i + 1) * HM // 16])
             nc.vector.tensor_tensor(sums[b, i][:, t, :], window, along[b, t][:, i * HM : (i + 1) * HM], ALU.add)
 
-        def root(b, i):
-            z_bf[b, i] = own_tile("zbf", b, i, [P, HM, PACK], BF16)
+        row_sums = {}
+
+        def pick_first(k):
+            pick_along(0, k)
+            row_sums[k] = own_tile("nsum", k, 0, [P, M], F32)
+            for i in range(2):
+                ms = slice(i * HM, (i + 1) * HM)
+                window = h_sq[0, k][:].indirect(pos2_t[:, i * HM // 16 : (i + 1) * HM // 16])
+                nc.vector.tensor_tensor(row_sums[k][:, ms], window, along[0, k][:, ms], ALU.add)
+
+        def deal_rows(k):
+            g, u = tiles[k]
+            slots = dealt[64 * g : 64 * (g + 1)].rearrange("q (e u) m -> q e u m", u=2)
+            nc.sync.dma_start(out=slots[:, :, u, :], in_=row_sums[k][:])
+
+        def root(b, i, rows):
+            z_bf[b, i] = own_tile("zbf", b, i, [P, rows.shape[2], PACK], BF16)
             nc.scalar.activation(
                 z_bf[b, i][:].rearrange("p (c u) t -> p c t u", u=4),
-                sums[b, i][:].rearrange("p t (c u) -> p c t u", u=4),
+                rows.rearrange("p t (c u) -> p c t u", u=4),
                 ACT.Sqrt,
             )
 
-        def quant_z(b, i):
-            z_codes[b, i] = own_tile("zcod", b, i, [P, HM], U32)
-            z_scales[b, i] = own_tile("zsc", b, i, [P, HM], U8)
+        def quant_z(b, i, width):
+            codes = own_tile("zcod", b, i, [P, width], U32)
+            scales = own_tile("zsc", b, i, [P, width], U8)
             nc.vector.quantize_mx(
-                out=z_codes[b, i][:].bitcast(FP8X4),
-                scales=z_scales[b, i][:],
-                in_=z_bf[b, i][:].rearrange("p m t -> p (m t)"),
+                out=codes[:].bitcast(FP8X4), scales=scales[:], in_=z_bf[b, i][:].rearrange("p m t -> p (m t)")
             )
+            for part in range(width // HM):
+                z_codes[b, i + part] = codes[:, part * HM : (part + 1) * HM]
+                z_scales[b, i + part] = scales[:, part * HM : (part + 1) * HM]
 
         y_acc = {}
 
@@ -213,74 +255,67 @@ def tile_list_putt_break_features_kernel(
 
         cast_w(0, 0, 0)
         gather_words(0)
-        load_w(1, 0)
         quant_w(0, 0)
         spread_base(0)
         spread_base(1)
         gather_words(1)
-        load_w(2, 0)
-        for t in range(PACK):
-            mm_h(0, 0, t)
-        gather_words(2)
-        load_w(0, 1)
-        cast_w(1, 0, 84)
-        load_w(1, 1)
+        cast_w(1, 0, 0)
         quant_w(1, 0)
-        cast_w(2, 0, 84)
-        load_w(2, 1)
-        quant_w(2, 0, 0, 1)
-        quant_w(2, 0, 1, 2)
-        quant_w(2, 0, 2, 4)
-        for t in range(PACK):
-            mm_h(1, 0, t)
-            mm_h(2, 0, t)
-
-        def pick_first(t):
-            pick_along(0, t)
-            pick_across(0, t, 0)
-            pick_across(0, t, 1)
-
+        gather_words(2)
+        cast_w(2, 0, 0)
+        quant_w(2, 0)
+        for k in range(2):
+            for a in range(KP):
+                mm_h(a, k)
+        for a in range(KP):
+            cast_w(a, 1, min(a, 1))
+            quant_w(a, 1)
+        slope_t = own_tile("slope", 0, 0, [P, NT, M], F32)
+        nc.sync.dma_start(out=slope_t[:], in_=slope.rearrange("(n p) m -> p n m", p=P))
         square_out(0, 0)
         pick_first(0)
         square_out(0, 1)
         pick_first(1)
-        cast_w(0, 1, 0)
-        slope_t = own_tile("slope", 0, 0, [P, NT, M], F32)
-        nc.sync.dma_start(out=slope_t[:], in_=slope.rearrange("(n p) m -> p n m", p=P))
-        quant_w(0, 1)
+        for a in range(KP):
+            mm_h(a, 2)
+            mm_h(a, 3)
         square_out(0, 2)
+        cast_w(0, 2, 0)
+        quant_w(0, 2)
+        cast_w(1, 2, 0)
+        quant_w(1, 2)
         pick_first(2)
-        cast_w(1, 1, 0)
+        dealt = own_tile("dealt", 0, 0, [P, PACK, M], F32)
+        for k in range(PACK - 1):
+            deal_rows(k)
         w4w_t = own_tile("w4w", 0, 0, [P, HP, 2 * N], U8)
         nc.sync.dma_start(out=w4w_t[:].bitcast(I32), in_=w4_words.rearrange("a p c -> p a c").bitcast(I32))
-        quant_w(1, 1)
-        cast_w(2, 1, 64)
-        quant_w(2, 1)
+        cast_w(2, 2, 0)
+        quant_w(2, 2)
         square_out(0, 3)
         pick_first(3)
+        deal_rows(3)
         for t in range(PACK):
             for a in range(KP):
-                mm_h(a, 1, t)
+                mm_h(a, PACK + t)
         for t in range(PACK):
             square_out(1, t)
             pick_along(1, t)
             pick_across(1, t, 0)
-            if t == 1:
-                for i in range(2):
-                    root(0, i)
-                    quant_z(0, i)
+        root(0, 0, dealt[:])
+        quant_z(0, 0, M)
         for i in range(2):
             for g in range(NT // 2):
                 mm_y(0, i, g)
-        root(1, 0)
-        quant_z(1, 0)
+        root(1, 0, sums[1, 0][:])
+        quant_z(1, 0, HM)
         for t in range(PACK):
             pick_across(1, t, 1)
-        root(1, 1)
+        root(1, 1, sums[1, 1][:])
         for g in range(NT // 2):
             mm_y(1, 0, g)
         finish(0, 0)
-        quant_z(1, 1)
+        quant_z(1, 1, HM)
         finish(0, 1)
         finish(0, 2)
         for g in range(NT // 2):

@@ -44,12 +44,13 @@ def tile_list_putt_break_features_kernel(
             ("tsc", 0, 0): 24 * KB, ("tab", 2, 0): 24 * KB, ("raw", 2, 0): 32 * KB,
             ("raw", 0, 1): 36 * KB, ("raw", 1, 1): 40 * KB, ("raw", 2, 1): 44 * KB,
             ("raw", 0, 2): 48 * KB, ("raw", 1, 2): 56 * KB, ("raw", 2, 2): 64 * KB,
-            ("slope", 0, 0): 36 * KB, ("w4w", 0, 0): 56 * KB, ("dealt", 0, 0): 48 * KB,
+            ("late", 0, 0): 24 * KB, ("late", 1, 0): 25 * KB, ("late", 2, 0): 26 * KB, ("vw", 2, 1): 32 * KB, ("slope", 0, 0): 36 * KB, ("w4w", 0, 0): 56 * KB, ("dealt", 0, 0): 48 * KB,
         }
         chains = [
-            [("codes", 2, 1), ("bf", 0, 2), ("along", 0, 2)],
+            [("codes", 2, 0), ("bf", 1, 1)],
+            [("latesc", 2, 0), ("bf", 0, 2), ("along", 0, 2)],
             [("wsc", 2, 1), ("bf", 1, 2), ("nsum", 2, 0)],
-            [("zbf", 0, 0), ("sums", 1, 1)],
+            [("zbf", 0, 1), ("sums", 1, 1)],
         ]
         shared = {}
         for i, chain in enumerate(chains):
@@ -72,7 +73,7 @@ def tile_list_putt_break_features_kernel(
         tsc_g = own_tile("tscg", 0, 0, [P, S], U8)
         v_scales = own_tile("vsc", 0, 0, [P, KP * S], U8)
         w4s_t = own_tile("w4s", 0, 0, [P, HP, N], U8)
-        v_words = [own_tile("vw", a, 0, [P, S], U16) for a in range(KP)]
+        v_words = {}
         base_t = [own_tile("base", b, 0, [P, PACK], F32) for b in range(HP)]
         warm_in = own_tile("warm", 0, 0, [P, 32], F32)
         warm_out = own_tile("warm", 1, 0, [P, 32], F32)
@@ -127,7 +128,15 @@ def tile_list_putt_break_features_kernel(
                 load_w(a, g)
 
         def gather_words(a):
-            nc.vector.tensor_copy(v_words[a][:], tab_t[a][:].indirect(offs_t[:]))
+            words = own_tile("vw", a, 0, [P, S], U16)
+            nc.vector.tensor_copy(words[:], tab_t[a][:].indirect(offs_t[:]))
+            for half in range(S // BANK):
+                v_words[a, half] = words[:, half * BANK : (half + 1) * BANK]
+
+        def gather_half(a, half):
+            words = own_tile("vw", a, half, [P, BANK], U16)
+            nc.vector.tensor_copy(words[:], tab_t[a][:].indirect(offs_t[:, half * BANK // 16 : (half + 1) * BANK // 16]))
+            v_words[a, half] = words[:]
 
         def cast_w(a, g, vector_share):
             d = deal[g]
@@ -144,28 +153,29 @@ def tile_list_putt_break_features_kernel(
             if split < runs:
                 nc.scalar.copy(dst[:, split:], src[:, split:])
 
-        def quant_w(a, g):
-            w_codes[a, g] = own_tile("codes", a, g, [P, deal[g] * P], U32)
-            w_scales[a, g] = own_tile("wsc", a, g, [P, deal[g] * P], U8)
+        def quant_w(a, g, t0=0, t1=None):
+            t1 = deal[g] if t1 is None else t1
+            codes = own_tile("late" if t0 else "codes", a, g, [P, (t1 - t0) * P], U32)
+            scales = own_tile("latesc" if t0 else "wsc", a, g, [P, (t1 - t0) * P], U8)
             nc.vector.quantize_mx(
-                out=w_codes[a, g][:].bitcast(FP8X4),
-                scales=w_scales[a, g][:],
-                in_=w_bf[a, g][:].rearrange("p t m j -> p (t m j)"),
+                out=codes[:].bitcast(FP8X4), scales=scales[:], in_=w_bf[a, g][:, t0:t1].rearrange("p t m j -> p (t m j)")
             )
+            for t in range(t0, t1):
+                w_codes[a, g, t] = codes[:, (t - t0) * P : (t - t0 + 1) * P]
+                w_scales[a, g, t] = scales[:, (t - t0) * P : (t - t0 + 1) * P]
 
         h_acc = {}
 
         def mm_h(a, k):
             g, t = tiles[k]
-            cols = slice(t * P, (t + 1) * P)
             for half in range(S // BANK):
                 if a == 0:
                     h_acc[k, half] = psum.tile([P, BANK], F32, name="acc", tag="acc")
                 nc.tensor.matmul_mx(
                     out=h_acc[k, half][:],
-                    lhsT=w_codes[a, g][:, cols].bitcast(FP8X4),
-                    lhsT_scale=w_scales[a, g][:, cols],
-                    rhs=v_words[a][:, half * BANK : (half + 1) * BANK].bitcast(FP4X4),
+                    lhsT=w_codes[a, g, t].bitcast(FP8X4),
+                    lhsT_scale=w_scales[a, g, t],
+                    rhs=v_words[a, half].bitcast(FP4X4),
                     rhs_scale=v_scales[:, a * S + half * BANK : a * S + (half + 1) * BANK],
                     start=(a == 0),
                     stop=(a == KP - 1),
@@ -255,24 +265,28 @@ def tile_list_putt_break_features_kernel(
 
         cast_w(0, 0, 0)
         gather_words(0)
-        quant_w(0, 0)
+        quant_w(0, 0, 0, 1)
         spread_base(0)
         spread_base(1)
         gather_words(1)
         cast_w(1, 0, 0)
-        quant_w(1, 0)
-        gather_words(2)
-        cast_w(2, 0, 0)
-        quant_w(2, 0)
-        for k in range(2):
-            for a in range(KP):
-                mm_h(a, k)
+        quant_w(1, 0, 0, 1)
+        gather_half(2, 0)
+        cast_w(2, 0, 1 / 2)
+        quant_w(2, 0, 0, 1)
+        gather_half(2, 1)
         for a in range(KP):
-            cast_w(a, 1, min(a, 1))
+            mm_h(a, 0)
+        for a in range(KP):
+            quant_w(a, 0, 1, 2)
+        for a in range(KP):
+            mm_h(a, 1)
+        square_out(0, 0)
+        for a in range(KP):
+            cast_w(a, 1, a // 2)
             quant_w(a, 1)
         slope_t = own_tile("slope", 0, 0, [P, NT, M], F32)
         nc.sync.dma_start(out=slope_t[:], in_=slope.rearrange("(n p) m -> p n m", p=P))
-        square_out(0, 0)
         pick_first(0)
         square_out(0, 1)
         pick_first(1)
@@ -302,11 +316,12 @@ def tile_list_putt_break_features_kernel(
             square_out(1, t)
             pick_along(1, t)
             pick_across(1, t, 0)
-        root(0, 0, dealt[:])
-        quant_z(0, 0, M)
-        for i in range(2):
-            for g in range(NT // 2):
-                mm_y(0, i, g)
+            if t >= 2:
+                i = t - 2
+                root(0, i, dealt[:, :, i * HM : (i + 1) * HM])
+                quant_z(0, i, HM)
+                for g in range(NT // 2):
+                    mm_y(0, i, g)
         root(1, 0, sums[1, 0][:])
         quant_z(1, 0, HM)
         for t in range(PACK):

from contextlib import ExitStack

import concourse.mybir as mybir

K, H, N, T, S, M = 1536, 1024, 768, 4096, 1024, 512
FLOPS = 2 * K * H * S + 2 * H * N * M

F32 = mybir.dt.float32
BF16 = mybir.dt.bfloat16
I32 = mybir.dt.int32
U32 = mybir.dt.uint32
U16 = mybir.dt.uint16
U8 = mybir.dt.uint8
FP8X4 = mybir.dt.float8_e4m3fn_x4
FP4X4 = mybir.dt.float4_e2m1fn_x4
ACT = mybir.ActivationFunctionType
ALU = mybir.AluOpType

P = 128
PACK = 4
PASS = P * PACK
KP = K // PASS
HP = H // PASS
BANK = 512
NT = N // P
HM = M // 2


def tile_list_putt_break_features_kernel(
    tc, tab_words, tab_scales, offs, pos1, pos2, w1, base, w4_words, w4_scales, slope, out
):
    nc = tc.nc
    with ExitStack() as ctx:
        keep = ctx.enter_context(tc.tile_pool(name="keep", bufs=1))
        stream = ctx.enter_context(tc.tile_pool(name="stream", bufs=1))
        psum = ctx.enter_context(tc.psum_pool(name="psum", bufs=8))

        offs_t = keep.tile([P, S // 16], U16, name="offs_t")
        pos1_t = keep.tile([P, M // 16], U16, name="pos1_t")
        pos2_t = keep.tile([P, M // 16], U16, name="pos2_t")
        KB = 1024
        placed = {
            ("warm", 0, 0): 0, ("tab", 0, 0): 0, ("warm", 1, 0): 16 * KB - 64, ("tab", 1, 0): 8 * KB, ("raw", 1, 0): 16 * KB,
            ("tsc", 0, 0): 24 * KB, ("tab", 2, 0): 24 * KB, ("raw", 2, 0): 32 * KB,
            ("raw", 0, 1): 36 * KB, ("raw", 1, 1): 40 * KB, ("raw", 2, 1): 44 * KB,
            ("raw", 0, 2): 48 * KB, ("raw", 1, 2): 56 * KB, ("raw", 2, 2): 64 * KB,
            ("late", 0, 0): 24 * KB, ("late", 1, 0): 25 * KB, ("late", 2, 0): 26 * KB, ("vw", 2, 1): 32 * KB, ("slope", 0, 0): 36 * KB, ("w4w", 0, 0): 56 * KB, ("dealt", 0, 0): 48 * KB,
        }
        chains = [
            [("codes", 2, 0), ("bf", 1, 1)],
            [("latesc", 2, 0), ("bf", 0, 2), ("along", 0, 2)],
            [("wsc", 2, 1), ("bf", 1, 2), ("nsum", 2, 0)],
            [("zbf", 0, 1), ("sums", 1, 1)],
        ]
        shared = {}
        for i, chain in enumerate(chains):
            for key in chain:
                shared[key] = "chain%d" % i

        def own_tile(kind, i, j, shape, dtype):
            name = "%s%d%d" % (kind, i, j)
            if (kind, i, j) in placed:
                return stream.tile(shape, dtype, name=name, tag=name, align_bytes=64, offset=placed[kind, i, j])
            tag = shared.get((kind, i, j), name)
            return keep.tile(shape, dtype, name=tag, tag=tag, align_bytes=64)

        first_col = (0, 256, 512)
        deal = (2, 2, 4)
        tiles = [(0, 0), (0, 1), (1, 0), (1, 1), (2, 0), (2, 1), (2, 2), (2, 3)]

        tab_t, w_raw, w_bf, w_codes, w_scales = {}, {}, {}, {}, {}
        tsc_t = own_tile("tsc", 0, 0, [P, 48 * KB], U8)
        tsc_g = own_tile("tscg", 0, 0, [P, S], U8)
        v_scales = own_tile("vsc", 0, 0, [P, KP * S], U8)
        w4s_t = own_tile("w4s", 0, 0, [P, HP, N], U8)
        v_words = {}
        base_t = [own_tile("base", b, 0, [P, PACK], F32) for b in range(HP)]
        warm_in = own_tile("warm", 0, 0, [P, 32], F32)
        warm_out = own_tile("warm", 1, 0, [P, 32], F32)

        def load_tab(a):
            tab_t[a] = own_tile("tab", a, 0, [P, T], U16)
            nc.sync.dma_start(out=tab_t[a][:].bitcast(I32), in_=tab_words[a].bitcast(I32))

        def load_w(a, g):
            width = deal[g] * P
            w_raw[a, g] = own_tile("raw", a, g, [P, PACK, width], F32)
            rows = w1[a * PASS : (a + 1) * PASS, first_col[g] : first_col[g] + width]
            nc.sync.dma_start(out=w_raw[a, g][:], in_=rows.rearrange("(p j) c -> p j c", j=PACK))

        nc.vector.memset(tsc_t[:, :T].bitcast(I32), 0)
        nc.vector.memset(v_scales[:].bitcast(I32), 0)
        nc.vector.memset(w4s_t[:].rearrange("p a c -> p (a c)").bitcast(I32), 0)
        nc.gpsimd.memset(warm_in[:], 1.0)
        nc.scalar.activation(warm_out[:], warm_in[:], ACT.Sqrt)

        nc.sync.dma_start(offs_t[:], offs)
        load_w(0, 0)
        nc.sync.dma_start(
            out=tsc_t[0:96:2, :T].bitcast(I32), in_=tab_scales.rearrange("a q t -> q a t").bitcast(I32)
        )
        nc.sync.dma_start(pos1_t[:], pos1)
        nc.sync.dma_start(pos2_t[:], pos2)
        nc.scalar.dma_start(
            out=base_t[0][:].rearrange("p (g u) -> p g u", u=2), in_=base[:PASS].rearrange("(g p u) -> p g u", p=P, u=2)
        )
        nc.scalar.dma_start(out=base_t[1][:], in_=base[PASS:].rearrange("(p t) -> p t", t=PACK))
        for q in range(4):
            nc.gpsimd.dma_start(
                out=w4s_t[32 * q : 32 * q + 4, :, :].bitcast(I32),
                in_=w4_scales[:, 4 * q : 4 * q + 4, :].rearrange("a r c -> r a c").bitcast(I32),
            )
        load_tab(0)
        load_tab(1)
        load_w(1, 0)

        nc.vector.tensor_copy(tsc_g[:], tsc_t[:, :T].indirect(offs_t[:]))
        for q in range(4):
            queue = nc.sync if q < 2 else nc.scalar
            queue.dma_start(
                out=v_scales[32 * q : 32 * q + 4, :].bitcast(I32),
                in_=tsc_g[24 * q : 24 * q + 24 : 2, :].bitcast(I32),
            )
        load_tab(2)
        load_w(2, 0)
        for g in range(1, 3):
            for a in range(KP):
                load_w(a, g)

        def gather_words(a):
            words = own_tile("vw", a, 0, [P, S], U16)
            nc.vector.tensor_copy(words[:], tab_t[a][:].indirect(offs_t[:]))
            for half in range(S // BANK):
                v_words[a, half] = words[:, half * BANK : (half + 1) * BANK]

        def gather_half(a, half):
            words = own_tile("vw", a, half, [P, BANK], U16)
            nc.vector.tensor_copy(words[:], tab_t[a][:].indirect(offs_t[:, half * BANK // 16 : (half + 1) * BANK // 16]))
            v_words[a, half] = words[:]

        def cast_w(a, g, vector_share):
            d = deal[g]
            w_bf[a, g] = own_tile("bf", a, g, [P, d, P, PACK], BF16)
            src = w_raw[a, g][:].rearrange("p j (c i t) -> p c j i t", i=PACK // d, t=d)
            dst = w_bf[a, g][:].rearrange("p t (c i) j -> p c j i t", i=PACK // d)
            if d == PACK:
                src = w_raw[a, g][:].rearrange("p j (c t) -> p c j t", t=d)
                dst = w_bf[a, g][:].rearrange("p t c j -> p c j t")
            runs = P * d // PACK
            split = 2 * round(runs * vector_share / 2)
            if split > 0:
                nc.vector.tensor_copy(dst[:, :split], src[:, :split])
            if split < runs:
                nc.scalar.copy(dst[:, split:], src[:, split:])

        def quant_w(a, g, t0=0, t1=None):
            t1 = deal[g] if t1 is None else t1
            codes = own_tile("late" if t0 else "codes", a, g, [P, (t1 - t0) * P], U32)
            scales = own_tile("latesc" if t0 else "wsc", a, g, [P, (t1 - t0) * P], U8)
            nc.vector.quantize_mx(
                out=codes[:].bitcast(FP8X4), scales=scales[:], in_=w_bf[a, g][:, t0:t1].rearrange("p t m j -> p (t m j)")
            )
            for t in range(t0, t1):
                w_codes[a, g, t] = codes[:, (t - t0) * P : (t - t0 + 1) * P]
                w_scales[a, g, t] = scales[:, (t - t0) * P : (t - t0 + 1) * P]

        h_acc = {}

        def mm_h(a, k):
            g, t = tiles[k]
            for half in range(S // BANK):
                if a == 0:
                    h_acc[k, half] = psum.tile([P, BANK], F32, name="acc", tag="acc")
                nc.tensor.matmul_mx(
                    out=h_acc[k, half][:],
                    lhsT=w_codes[a, g, t].bitcast(FP8X4),
                    lhsT_scale=w_scales[a, g, t],
                    rhs=v_words[a, half].bitcast(FP4X4),
                    rhs_scale=v_scales[:, a * S + half * BANK : a * S + (half + 1) * BANK],
                    start=(a == 0),
                    stop=(a == KP - 1),
                )

        base_w, h_sq, along, sums, z_bf, z_codes, z_scales = {}, {}, {}, {}, {}, {}, {}

        def spread_base(b):
            base_w[b] = own_tile("basew", b, 0, [P, PACK, HM], F32)
            nc.scalar.copy(base_w[b][:], base_t[b][:].unsqueeze(2).to_broadcast([P, PACK, HM]))

        def square_out(b, t):
            h_sq[b, t] = own_tile("hsq", b, t, [P, S], F32)
            for half in range(S // BANK):
                nc.scalar.activation(h_sq[b, t][:, half * BANK : (half + 1) * BANK], h_acc[PACK * b + t, half][:], ACT.Square)

        def pick_along(b, t):
            along[b, t] = own_tile("along", b, t, [P, M], F32)
            for i in range(2):
                window = h_sq[b, t][:].indirect(pos1_t[:, i * HM // 16 : (i + 1) * HM // 16])
                nc.vector.tensor_tensor(along[b, t][:, i * HM : (i + 1) * HM], window, base_w[b][:, t, :], ALU.add)

        def pick_across(b, t, i):
            if t == 0:
                sums[b, i] = own_tile("sums", b, i, [P, PACK, HM], F32)
            window = h_sq[b, t][:].indirect(pos2_t[:, i * HM // 16 : (i + 1) * HM // 16])
            nc.vector.tensor_tensor(sums[b, i][:, t, :], window, along[b, t][:, i * HM : (i + 1) * HM], ALU.add)

        row_sums = {}

        def pick_first(k):
            pick_along(0, k)
            row_sums[k] = own_tile("nsum", k, 0, [P, M], F32)
            for i in range(2):
                ms = slice(i * HM, (i + 1) * HM)
                window = h_sq[0, k][:].indirect(pos2_t[:, i * HM // 16 : (i + 1) * HM // 16])
                nc.vector.tensor_tensor(row_sums[k][:, ms], window, along[0, k][:, ms], ALU.add)

        def deal_rows(k):
            g, u = tiles[k]
            slots = dealt[64 * g : 64 * (g + 1)].rearrange("q (e u) m -> q e u m", u=2)
            nc.sync.dma_start(out=slots[:, :, u, :], in_=row_sums[k][:])

        def root(b, i, rows):
            z_bf[b, i] = own_tile("zbf", b, i, [P, rows.shape[2], PACK], BF16)
            nc.scalar.activation(
                z_bf[b, i][:].rearrange("p (c u) t -> p c t u", u=4),
                rows.rearrange("p t (c u) -> p c t u", u=4),
                ACT.Sqrt,
            )

        def quant_z(b, i, width):
            codes = own_tile("zcod", b, i, [P, width], U32)
            scales = own_tile("zsc", b, i, [P, width], U8)
            nc.vector.quantize_mx(
                out=codes[:].bitcast(FP8X4), scales=scales[:], in_=z_bf[b, i][:].rearrange("p m t -> p (m t)")
            )
            for part in range(width // HM):
                z_codes[b, i + part] = codes[:, part * HM : (part + 1) * HM]
                z_scales[b, i + part] = scales[:, part * HM : (part + 1) * HM]

        y_acc = {}

        def mm_y(b, i, g):
            if b == 0:
                y_acc[i, g] = psum.tile([P, 2, HM], F32, name="acc", tag="acc")
            for u in range(2):
                n = 2 * g + u
                for c in range(HM // P):
                    cols = slice(c * P, (c + 1) * P)
                    nc.tensor.matmul_mx(
                        out=y_acc[i, g][:, u, cols],
                        lhsT=w4w_t[:, b, 2 * n * P : 2 * (n + 1) * P].bitcast(FP4X4),
                        lhsT_scale=w4s_t[:, b, n * P : (n + 1) * P],
                        rhs=z_codes[b, i][:, cols].bitcast(FP8X4),
                        rhs_scale=z_scales[b, i][:, cols],
                        start=(b == 0 and u == 0 and c == 0),
                        stop=(b == HP - 1 and u == 1 and c == HM // P - 1),
                    )

        def finish(i, g):
            ms = slice(i * HM, (i + 1) * HM)
            res = own_tile("res", i, g, [P, 2, HM], F32)
            nc.vector.tensor_tensor(res[:], y_acc[i, g][:], slope_t[:, 2 * g : 2 * g + 2, ms], ALU.subtract)
            rows = out[2 * g * P : (2 * g + 2) * P, ms]
            nc.sync.dma_start(out=rows.rearrange("(u p) m -> p u m", p=P), in_=res[:])

        cast_w(0, 0, 0)
        gather_words(0)
        quant_w(0, 0, 0, 1)
        spread_base(0)
        spread_base(1)
        gather_words(1)
        cast_w(1, 0, 0)
        quant_w(1, 0, 0, 1)
        gather_half(2, 0)
        cast_w(2, 0, 1 / 2)
        quant_w(2, 0, 0, 1)
        gather_half(2, 1)
        for a in range(KP):
            mm_h(a, 0)
        for a in range(KP):
            quant_w(a, 0, 1, 2)
        for a in range(KP):
            mm_h(a, 1)
        square_out(0, 0)
        for a in range(KP):
            cast_w(a, 1, a // 2)
            quant_w(a, 1)
        slope_t = own_tile("slope", 0, 0, [P, NT, M], F32)
        nc.sync.dma_start(out=slope_t[:], in_=slope.rearrange("(n p) m -> p n m", p=P))
        pick_first(0)
        square_out(0, 1)
        pick_first(1)
        for a in range(KP):
            mm_h(a, 2)
            mm_h(a, 3)
        square_out(0, 2)
        cast_w(0, 2, 0)
        quant_w(0, 2)
        cast_w(1, 2, 0)
        quant_w(1, 2)
        pick_first(2)
        dealt = own_tile("dealt", 0, 0, [P, PACK, M], F32)
        for k in range(PACK - 1):
            deal_rows(k)
        w4w_t = own_tile("w4w", 0, 0, [P, HP, 2 * N], U8)
        nc.sync.dma_start(out=w4w_t[:].bitcast(I32), in_=w4_words.rearrange("a p c -> p a c").bitcast(I32))
        cast_w(2, 2, 0)
        quant_w(2, 2)
        square_out(0, 3)
        pick_first(3)
        deal_rows(3)
        for t in range(PACK):
            for a in range(KP):
                mm_h(a, PACK + t)
        for t in range(PACK):
            square_out(1, t)
            pick_along(1, t)
            pick_across(1, t, 0)
            if t >= 2:
                i = t - 2
                root(0, i, dealt[:, :, i * HM : (i + 1) * HM])
                quant_z(0, i, HM)
                for g in range(NT // 2):
                    mm_y(0, i, g)
        root(1, 0, sums[1, 0][:])
        quant_z(1, 0, HM)
        for t in range(PACK):
            pick_across(1, t, 1)
        root(1, 1, sums[1, 1][:])
        for g in range(NT // 2):
            mm_y(1, 0, g)
        finish(0, 0)
        quant_z(1, 1, HM)
        finish(0, 1)
        finish(0, 2)
        for g in range(NT // 2):
            mm_y(1, 1, g)
            finish(1, g)
